import numpy as np
import ml_dtypes


def mxq(x, axis, fmt="e4m3"):
    dtype, down = {"e4m3": (ml_dtypes.float8_e4m3fn, 7), "e5m2": (ml_dtypes.float8_e5m2, 14)}[fmt]
    v = np.moveaxis(np.asarray(x, np.float32).astype(ml_dtypes.bfloat16).astype(np.float64), axis, -1)
    blocks = v.reshape(v.shape[:-1] + (-1, 32))
    amax = np.abs(blocks).max(-1, keepdims=True)
    byte = np.maximum(np.where(amax > 0, np.frexp(amax)[1] - 1 + 127, 0) - down, 1)
    scale = np.exp2(byte - 127.0)
    codes = (blocks / scale).astype(np.float32).astype(dtype).astype(np.float64)
    return np.moveaxis((codes * scale).reshape(v.shape), -1, axis)


WIDE = False


def mx_kscale(k):
    if not WIDE:
        return np.ones(k)
    levels = np.array([10, -10, 5, -5, 0])
    if k % 512:
        return np.exp2(np.random.permutation(np.resize(levels, k // 32))).repeat(32)
    a = np.empty((k // 512, 16))
    for p in range(k // 512):
        a[p, :8] = np.random.permutation(np.resize(levels, 8))
        for g in range(8):
            far = levels[np.abs(levels - a[p, g]) >= 10]
            a[p, g + 8] = far[np.random.randint(len(far))]
    return np.exp2(a.ravel()).repeat(32)


def f64(x):
    return np.asarray(x).astype(np.float64)


def striped(idx):
    return np.tile(idx.reshape(-1, 16).T, (8, 1)).astype(np.uint16)


def unstriped(offs):
    return offs[:16].T.reshape(-1).astype(np.int64)


def striped8(idx):
    return np.concatenate([x.reshape(-1, 16).T for x in idx]).astype(np.uint16)


def runs(offs, k):
    lists = np.stack([offs[16 * r : 16 * r + 16].T.reshape(-1) for r in range(8)]).astype(np.int64)
    return lists[np.arange(k) % 512 // 64]


def pack_weight(w):
    k, n = w.shape
    w = f64(np.asarray(w, np.float32).astype(ml_dtypes.bfloat16)).reshape(k // 32, 32, n)
    amax = np.abs(w).max(1)
    byte = np.clip(np.where(amax > 0, np.frexp(amax)[1] - 1 + 127 - 7, 1), 1, 254)
    scaled = (w * np.exp2(127.0 - byte)[:, None, :]).reshape(k, n).astype(np.float32)
    words = np.ascontiguousarray(scaled.reshape(k // 512, 128, 4, n).transpose(0, 1, 3, 2)).astype(ml_dtypes.float8_e4m3fn).view(np.uint8)
    return words, np.ascontiguousarray(byte.astype(np.uint8).reshape(k // 512, 16, n))


def unpack_weight(words, scales):
    g, p, n, _ = words.shape
    vals = np.ascontiguousarray(words).view(ml_dtypes.float8_e4m3fn).astype(np.float64) * np.repeat(np.exp2(scales.astype(np.float64) - 127.0), 8, axis=1)[..., None]
    return vals.transpose(0, 1, 3, 2).reshape(g * 512, n)


K, T, S, N, H, W = 512, 2048, 512, 512, 512, 256


def setup_inputs():
    n = np.random.standard_normal
    s = mx_kscale(K)[:, None]
    u = mx_kscale(H)
    packed_xT = pack_weight(n((K, T)) * s)
    return {
        "x_words": packed_xT[0],
        "x_scales": packed_xT[1],
        "w1": (n((K, H)) / np.sqrt(K) / s).astype(np.float32),
        "gn": (np.random.uniform(0.5, 1.5, (H, 1)) * u[:, None]).astype(np.float32),
        "w2": (n((H, N)) / np.sqrt(H) / u[:, None]).astype(np.float32),
        "offs": striped(np.random.permutation(T)[:S]),
        "n1": striped8(np.stack([np.random.permutation(S) for _ in range(8)])),
        "n2": striped8(np.stack([np.random.permutation(S) for _ in range(8)])),
        "n3": striped8(np.stack([np.random.permutation(S)[:W] for _ in range(8)])),
        "n4": striped8(np.stack([np.random.permutation(S)[:W] for _ in range(8)])),
    }


def reference(x_words, x_scales, w1, gn, w2, offs, n1, n2, n3, n4):
    xq = unpack_weight(x_words, x_scales)[:, unstriped(offs)]
    y = mxq(f64(w1), 0, "e4m3").T @ xq
    st = y + 0.5 * (y[np.arange(H)[:, None], runs(n1, H)])
    z = f64(gn) * (st - (st[np.arange(H)[:, None], runs(n2, H)]))
    h = mxq(f64(w2), 0, "e4m3").T @ mxq(z, 0, "e4m3")
    ra = y[np.arange(H)[:, None], runs(n4, H)] - (0.5 * (h[np.arange(N)[:, None], runs(n3, N)]))
    out = h.copy()
    out[np.arange(H)[:, None], runs(n3, H)] = ra
    return out

@@ -1,0 +1,189 @@
+from contextlib import ExitStack
+
+import concourse.mybir as mybir
+
+K, T, S, N, H, W = 512, 2048, 512, 512, 512, 256
+FLOPS = 2 * K * H * S + 2 * H * N * S
+
+F32 = mybir.dt.float32
+BF16 = mybir.dt.bfloat16
+I32 = mybir.dt.int32
+U32 = mybir.dt.uint32
+U16 = mybir.dt.uint16
+U8 = mybir.dt.uint8
+FP8X4 = mybir.dt.float8_e4m3fn_x4
+COPY = mybir.ActivationFunctionType.Copy
+ADD = mybir.AluOpType.add
+SUB = mybir.AluOpType.subtract
+MULT = mybir.AluOpType.mult
+
+P = 128
+PACK = 4
+HALF = S // 2
+LIST_HALF = HALF // 16
+
+
+def tile_picked_skipputbhop_none_p_kernel(
+    tc, x_words, x_scales, w1, gn, w2, offs, n1, n2, n3, n4, out
+):
+    nc = tc.nc
+    halves = [slice(a * HALF, (a + 1) * HALF) for a in range(2)]
+    list_halves = [slice(a * LIST_HALF, (a + 1) * LIST_HALF) for a in range(2)]
+    with ExitStack() as ctx:
+        keep = ctx.enter_context(tc.tile_pool(name="keep", bufs=1))
+        psum = ctx.enter_context(tc.psum_pool(name="psum", bufs=1))
+
+        def sb(name, shape, dtype, tag=None):
+            return keep.tile(shape, dtype, name=name, tag=tag or name, align_bytes=64)
+
+        def load_list(name, src):
+            tile = keep.tile(list(src.shape), U16, name=name)
+            nc.sync.dma_start(tile[:], src)
+            return tile
+
+        def deal(engine_copy, dealt, raw, a):
+            engine_copy(
+                dealt[:, :, a * (P // 2) : (a + 1) * (P // 2), :].rearrange("p t m j -> p m j t"),
+                raw[:, :, halves[a]].rearrange("p j (m t) -> p m j t", t=PACK),
+            )
+
+        def product(acc, codes, scales, t, rhs_codes, rhs_scales):
+            nc.tensor.matmul_mx(
+                out=acc,
+                lhsT=codes[:, t * P : (t + 1) * P].bitcast(FP8X4),
+                lhsT_scale=scales[:, t * P : (t + 1) * P],
+                rhs=rhs_codes.bitcast(FP8X4),
+                rhs_scale=rhs_scales,
+                start=True,
+                stop=True,
+            )
+
+        scale_rows = sb("scale_rows", [P, T], U8)
+        nc.vector.memset(scale_rows[:].bitcast(I32), 0)
+        for q in range(4):
+            nc.sync.dma_start(
+                scale_rows[32 * q : 32 * q + 4, :].bitcast(I32), x_scales[0, 4 * q : 4 * q + 4, :].bitcast(I32)
+            )
+        offs_sb = load_list("offs_sb", offs)
+        n1_sb = load_list("n1_sb", n1)
+        n2_sb = load_list("n2_sb", n2)
+        w1_raw = sb("w1_raw", [P, PACK, H], F32, tag="w_raw")
+        nc.sync.dma_start(w1_raw[:], w1.rearrange("(p j) c -> p j c", j=PACK))
+        n4_sb = load_list("n4_sb", n4)
+        n3_sb = load_list("n3_sb", n3)
+        words = sb("words", [P, T], I32)
+        nc.sync.dma_start(words[:], x_words[0].rearrange("p c r -> p (c r)").bitcast(I32))
+        gain = sb("gain", [P, PACK], F32)
+        nc.sync.dma_start(gain[:], gn.rearrange("(p t) o -> p (t o)", t=PACK))
+
+        w1_cols = w1_raw[:].rearrange("p j (m t) -> p m j t", t=PACK)
+        w1_first = sb("w1_first", [P, P, PACK], BF16)
+        nc.vector.tensor_copy(w1_first[:], w1_cols[:, :, :, 0])
+        w1_rest = sb("w1_rest", [P, PACK - 1, P, PACK], BF16)
+        nc.scalar.copy(w1_rest[:].rearrange("p t m j -> p m j t"), w1_cols[:, :, :, 1:PACK])
+        w1_codes = sb("w1_codes", [P, H], U32)
+        w1_scales = sb("w1_scales", [P, H], U8)
+
+        def quantize_w1(t, src):
+            nc.vector.quantize_mx(
+                out=w1_codes[:, t * P : (t + 1) * P].bitcast(FP8X4),
+                scales=w1_scales[:, t * P : (t + 1) * P],
+                in_=src.rearrange("p m j -> p (m j)"),
+            )
+
+        quantize_w1(0, w1_first[:])
+        x_bytes = sb("x_bytes", [P, S], U8, tag="w1_first")
+        nc.vector.tensor_copy(x_bytes[:], scale_rows[:].indirect(offs_sb[:]))
+        w2_raw = sb("w2_raw", [P, PACK, N], F32, tag="w_raw")
+        nc.sync.dma_start(w2_raw[:], w2.rearrange("(p j) c -> p j c", j=PACK))
+
+        gain_neg = sb("gain_neg", [P, PACK], F32)
+        gain_neg_half = sb("gain_neg_half", [P, PACK], F32)
+        nc.scalar.activation(gain_neg[:], gain[:], COPY, scale=-1.0)
+        nc.scalar.activation(gain_neg_half[:], gain[:], COPY, scale=-0.5)
+
+        x_codes = sb("x_codes", [P, S], U32)
+        for a in range(2):
+            nc.vector.tensor_copy(x_codes[:, halves[a]], words[:].bitcast(U32).indirect(offs_sb[:, list_halves[a]]))
+
+        for t in range(1, PACK):
+            quantize_w1(t, w1_rest[:, t - 1, :, :])
+
+        y_parts = []
+        for t in range(PACK):
+            spans = halves if t == 0 else [slice(0, S)]
+            parts = []
+            for a, cols in enumerate(spans):
+                bank = psum.tile([P, cols.stop - cols.start], F32, name="y_ps%d_%d" % (t, a), tag="bank%d" % (t + PACK * a))
+                product(bank[:], w1_codes, w1_scales, t, x_codes[:, cols], x_bytes[:, cols])
+                parts.append((bank, cols))
+            y_parts.append(parts)
+
+        st = [sb("st%d" % t, [P, S], F32) for t in range(PACK)]
+        for t in range(PACK):
+            gy_half = sb("gy_half%d" % t, [P, S], F32)
+            gy = sb("gy%d" % t, [P, S], F32)
+            for bank, cols in y_parts[t]:
+                nc.scalar.activation(gy_half[:, cols], bank[:], COPY, scale=gain_neg_half[:, t : t + 1])
+            for bank, cols in y_parts[t]:
+                nc.scalar.activation(gy[:, cols], bank[:], COPY, scale=gain_neg[:, t : t + 1])
+            for a in range(2):
+                nc.vector.tensor_tensor(st[t][:, halves[a]], gy_half[:].indirect(n1_sb[:, list_halves[a]]), gy[:, halves[a]], ADD)
+        st_copy = [sb("st_copy%d" % t, [P, S], F32) for t in range(PACK)]
+        for t in range(PACK):
+            nc.scalar.copy(st_copy[t][:], st[t][:])
+
+        w2_bf = sb("w2_bf", [P, PACK, P, PACK], BF16)
+        for a in range(2):
+            deal(nc.scalar.copy, w2_bf, w2_raw, a)
+
+        z32 = [sb("z32_%d" % a, [P, PACK, HALF], F32) for a in range(2)]
+        z_bf = [sb("z_bf%d" % a, [P, HALF, PACK], BF16) for a in range(2)]
+        for a in range(2):
+            for t in range(PACK):
+                nc.vector.tensor_tensor(z32[a][:, t, :], st[t][:].indirect(n2_sb[:, list_halves[a]]), st_copy[t][:, halves[a]], SUB)
+
+        w2_codes = sb("w2_codes", [P, N], U32)
+        w2_scales = sb("w2_scales", [P, N], U8)
+        nc.vector.quantize_mx(
+            out=w2_codes[:].bitcast(FP8X4), scales=w2_scales[:], in_=w2_bf[:].rearrange("p t m j -> p (t m j)")
+        )
+
+        z_codes = sb("z_codes", [P, S], U32)
+        z_scales = sb("z_scales", [P, S], U8)
+        y_picked = [sb("y_picked%d" % t, [P, W], F32) for t in range(PACK)]
+        for a in range(2):
+            nc.scalar.copy(
+                z_bf[a][:].rearrange("p (c i) t -> p c t i", i=4), z32[a][:].rearrange("p t (c i) -> p c t i", i=4)
+            )
+            nc.vector.quantize_mx(
+                out=z_codes[:, halves[a]].bitcast(FP8X4),
+                scales=z_scales[:, halves[a]],
+                in_=z_bf[a][:].rearrange("p c t -> p (c t)"),
+            )
+            for t in (2 * a, 2 * a + 1):
+                y_sb = sb("y_sb%d" % t, [P, S], F32, tag="st_copy%d" % t)
+                for bank, cols in y_parts[t]:
+                    nc.scalar.copy(y_sb[:, cols], bank[:])
+                nc.vector.tensor_copy(y_picked[t][:], y_sb[:].indirect(n4_sb[:]))
+
+        out_rows = out.rearrange("(p t) c -> p t c", t=PACK)
+        h_sb = [sb("h_sb%d" % t, [P, S], F32) for t in range(PACK)]
+        h_picked = [sb("h_picked%d" % t, [P, W], F32) for t in range(PACK)]
+        for t in range(PACK):
+            h_ps = psum.tile([P, S], F32, name="h_ps%d" % t, tag="bank%d" % ((5 + t) % 8))
+            product(h_ps[:], w2_codes, w2_scales, t, z_codes[:], z_scales[:])
+            nc.scalar.copy(h_sb[t][:], h_ps[:])
+
+        def fetch(t):
+            nc.vector.tensor_scalar(h_picked[t][:], h_sb[t][:].indirect(n3_sb[:]), -0.5, 0.0, MULT, ADD)
+
+        def put(t):
+            nc.vector.tensor_tensor(h_sb[t][:].indirect(n3_sb[:]), y_picked[t][:], h_picked[t][:], ADD)
+            nc.sync.dma_start(out_rows[:, t, :], h_sb[t][:])
+
+        fetch(0)
+        for t in range(PACK):
+            if t + 1 < PACK:
+                fetch(t + 1)
+            put(t)

@@ -50,7 +50,7 @@ def tile_picked_skipputbhop_none_p_kernel(
         def product(acc, codes, scales, t, rhs_codes, rhs_scales):
             nc.tensor.matmul_mx(
                 out=acc,
-                lhsT=codes[:, t * P : (t + 1) * P].bitcast(FP8X4),
+                lhsT=codes.bitcast(FP8X4),
                 lhsT_scale=scales[:, t * P : (t + 1) * P],
                 rhs=rhs_codes.bitcast(FP8X4),
                 rhs_scale=rhs_scales,
@@ -60,38 +60,30 @@ def tile_picked_skipputbhop_none_p_kernel(
 
         scale_rows = sb("scale_rows", [P, T], U8)
         nc.vector.memset(scale_rows[:].bitcast(I32), 0)
-        for q in range(4):
-            nc.sync.dma_start(
-                scale_rows[32 * q : 32 * q + 4, :].bitcast(I32), x_scales[0, 4 * q : 4 * q + 4, :].bitcast(I32)
-            )
-        offs_sb = load_list("offs_sb", offs)
-        n1_sb = load_list("n1_sb", n1)
-        n2_sb = load_list("n2_sb", n2)
+        for r in range(4):
+            nc.sync.dma_start(scale_rows[r:P:32, :].bitcast(I32), x_scales[0, r:16:4, :].bitcast(I32))
         w1_raw = sb("w1_raw", [P, PACK, H], F32, tag="w_raw")
         nc.sync.dma_start(w1_raw[:], w1.rearrange("(p j) c -> p j c", j=PACK))
-        n4_sb = load_list("n4_sb", n4)
-        n3_sb = load_list("n3_sb", n3)
-        words = sb("words", [P, T], I32)
-        nc.sync.dma_start(words[:], x_words[0].rearrange("p c r -> p (c r)").bitcast(I32))
+        offs_sb = load_list("offs_sb", offs)
         gain = sb("gain", [P, PACK], F32)
         nc.sync.dma_start(gain[:], gn.rearrange("(p t) o -> p (t o)", t=PACK))
+        words = sb("words", [P, T], I32)
+        nc.sync.dma_start(words[:], x_words[0].rearrange("p c r -> p (c r)").bitcast(I32))
+        n1_sb = load_list("n1_sb", n1)
+        n2_sb = load_list("n2_sb", n2)
+        n4_sb = load_list("n4_sb", n4)
+        n3_sb = load_list("n3_sb", n3)
 
         w1_cols = w1_raw[:].rearrange("p j (m t) -> p m j t", t=PACK)
         w1_first = sb("w1_first", [P, P, PACK], BF16)
         nc.vector.tensor_copy(w1_first[:], w1_cols[:, :, :, 0])
         w1_rest = sb("w1_rest", [P, PACK - 1, P, PACK], BF16)
         nc.scalar.copy(w1_rest[:].rearrange("p t m j -> p m j t"), w1_cols[:, :, :, 1:PACK])
-        w1_codes = sb("w1_codes", [P, H], U32)
         w1_scales = sb("w1_scales", [P, H], U8)
-
-        def quantize_w1(t, src):
-            nc.vector.quantize_mx(
-                out=w1_codes[:, t * P : (t + 1) * P].bitcast(FP8X4),
-                scales=w1_scales[:, t * P : (t + 1) * P],
-                in_=src.rearrange("p m j -> p (m j)"),
-            )
-
-        quantize_w1(0, w1_first[:])
+        first_codes = sb("first_codes", [P, P], U32)
+        nc.vector.quantize_mx(
+            out=first_codes[:].bitcast(FP8X4), scales=w1_scales[:, 0:P], in_=w1_first[:].rearrange("p m j -> p (m j)")
+        )
         x_bytes = sb("x_bytes", [P, S], U8, tag="w1_first")
         nc.vector.tensor_copy(x_bytes[:], scale_rows[:].indirect(offs_sb[:]))
         w2_raw = sb("w2_raw", [P, PACK, N], F32, tag="w_raw")
@@ -106,8 +98,14 @@ def tile_picked_skipputbhop_none_p_kernel(
         for a in range(2):
             nc.vector.tensor_copy(x_codes[:, halves[a]], words[:].bitcast(U32).indirect(offs_sb[:, list_halves[a]]))
 
+        rest_codes = sb("rest_codes", [P, H - P], U32, tag="words")
+        w1_codes = [first_codes[:]] + [rest_codes[:, (t - 1) * P : t * P] for t in range(1, PACK)]
         for t in range(1, PACK):
-            quantize_w1(t, w1_rest[:, t - 1, :, :])
+            nc.vector.quantize_mx(
+                out=w1_codes[t].bitcast(FP8X4),
+                scales=w1_scales[:, t * P : (t + 1) * P],
+                in_=w1_rest[:, t - 1, :, :].rearrange("p m j -> p (m j)"),
+            )
 
         y_parts = []
         for t in range(PACK):
@@ -115,23 +113,27 @@ def tile_picked_skipputbhop_none_p_kernel(
             parts = []
             for a, cols in enumerate(spans):
                 bank = psum.tile([P, cols.stop - cols.start], F32, name="y_ps%d_%d" % (t, a), tag="bank%d" % (t + PACK * a))
-                product(bank[:], w1_codes, w1_scales, t, x_codes[:, cols], x_bytes[:, cols])
+                product(bank[:], w1_codes[t], w1_scales, t, x_codes[:, cols], x_bytes[:, cols])
                 parts.append((bank, cols))
             y_parts.append(parts)
 
         st = [sb("st%d" % t, [P, S], F32) for t in range(PACK)]
         for t in range(PACK):
-            gy_half = sb("gy_half%d" % t, [P, S], F32)
+            gy_half = sb("gy_half%d" % t, [P, S if t == 0 else 2 * S], F32)
+            if t > 0:
+                nc.gpsimd.memset(gy_half[:, S:], 0.0)
             gy = sb("gy%d" % t, [P, S], F32)
             for bank, cols in y_parts[t]:
                 nc.scalar.activation(gy_half[:, cols], bank[:], COPY, scale=gain_neg_half[:, t : t + 1])
             for bank, cols in y_parts[t]:
                 nc.scalar.activation(gy[:, cols], bank[:], COPY, scale=gain_neg[:, t : t + 1])
-            for a in range(2):
-                nc.vector.tensor_tensor(st[t][:, halves[a]], gy_half[:].indirect(n1_sb[:, list_halves[a]]), gy[:, halves[a]], ADD)
+            for bank, cols in y_parts[t]:
+                entries = slice(cols.start // 16, cols.stop // 16)
+                nc.vector.tensor_tensor(st[t][:, cols], gy_half[:].indirect(n1_sb[:, entries]), gy[:, cols], ADD)
         st_copy = [sb("st_copy%d" % t, [P, S], F32) for t in range(PACK)]
-        for t in range(PACK):
-            nc.scalar.copy(st_copy[t][:], st[t][:])
+        for t in range(PACK - 1):
+            nc.sync.dma_start(st_copy[t][:], st[t][:])
+        nc.scalar.copy(st_copy[PACK - 1][:], st[PACK - 1][:])
 
         w2_bf = sb("w2_bf", [P, PACK, P, PACK], BF16)
         for a in range(2):
@@ -172,7 +174,7 @@ def tile_picked_skipputbhop_none_p_kernel(
         h_picked = [sb("h_picked%d" % t, [P, W], F32) for t in range(PACK)]
         for t in range(PACK):
             h_ps = psum.tile([P, S], F32, name="h_ps%d" % t, tag="bank%d" % ((5 + t) % 8))
-            product(h_ps[:], w2_codes, w2_scales, t, z_codes[:], z_scales[:])
+            product(h_ps[:], w2_codes[:, t * P : (t + 1) * P], w2_scales, t, z_codes[:], z_scales[:])
             nc.scalar.copy(h_sb[t][:], h_ps[:])
 
         def fetch(t):

@@ -62,7 +62,7 @@ def tile_picked_skipputbhop_none_p_kernel(
         nc.vector.memset(scale_rows[:].bitcast(I32), 0)
         for r in range(4):
             nc.sync.dma_start(scale_rows[r:P:32, :].bitcast(I32), x_scales[0, r:16:4, :].bitcast(I32))
-        w1_raw = sb("w1_raw", [P, PACK, H], F32, tag="w_raw")
+        w1_raw = sb("w1_raw", [P, PACK, H], F32)
         nc.sync.dma_start(w1_raw[:], w1.rearrange("(p j) c -> p j c", j=PACK))
         offs_sb = load_list("offs_sb", offs)
         gain = sb("gain", [P, PACK], F32)
@@ -70,6 +70,8 @@ def tile_picked_skipputbhop_none_p_kernel(
         words = sb("words", [P, T], I32)
         nc.sync.dma_start(words[:], x_words[0].rearrange("p c r -> p (c r)").bitcast(I32))
         n1_sb = load_list("n1_sb", n1)
+        w2_raw = sb("w2_raw", [P, PACK, N], F32)
+        nc.sync.dma_start(w2_raw[:], w2.rearrange("(p j) c -> p j c", j=PACK))
         n2_sb = load_list("n2_sb", n2)
         n4_sb = load_list("n4_sb", n4)
         n3_sb = load_list("n3_sb", n3)
@@ -86,8 +88,6 @@ def tile_picked_skipputbhop_none_p_kernel(
         )
         x_bytes = sb("x_bytes", [P, S], U8, tag="w1_first")
         nc.vector.tensor_copy(x_bytes[:], scale_rows[:].indirect(offs_sb[:]))
-        w2_raw = sb("w2_raw", [P, PACK, N], F32, tag="w_raw")
-        nc.sync.dma_start(w2_raw[:], w2.rearrange("(p j) c -> p j c", j=PACK))
 
         gain_neg = sb("gain_neg", [P, PACK], F32)
         gain_neg_half = sb("gain_neg_half", [P, PACK], F32)
@@ -121,31 +121,33 @@ def tile_picked_skipputbhop_none_p_kernel(
         for t in range(PACK):
             gy_half = sb("gy_half%d" % t, [P, S if t == 0 else 2 * S], F32)
             if t > 0:
-                nc.gpsimd.memset(gy_half[:, S:], 0.0)
+                nc.vector.memset(gy_half[:, S:], 0.0)
             gy = sb("gy%d" % t, [P, S], F32)
             for bank, cols in y_parts[t]:
                 nc.scalar.activation(gy_half[:, cols], bank[:], COPY, scale=gain_neg_half[:, t : t + 1])
-            for bank, cols in y_parts[t]:
                 nc.scalar.activation(gy[:, cols], bank[:], COPY, scale=gain_neg[:, t : t + 1])
             for bank, cols in y_parts[t]:
                 entries = slice(cols.start // 16, cols.stop // 16)
                 nc.vector.tensor_tensor(st[t][:, cols], gy_half[:].indirect(n1_sb[:, entries]), gy[:, cols], ADD)
-        st_copy = [sb("st_copy%d" % t, [P, S], F32) for t in range(PACK)]
+        left = sb("left", [P, PACK, HALF], F32)
+        right = [sb("right%d" % t, [P, HALF], F32, tag="st_copy%d" % t) for t in range(PACK)]
         for t in range(PACK - 1):
-            nc.sync.dma_start(st_copy[t][:], st[t][:])
-        nc.scalar.copy(st_copy[PACK - 1][:], st[PACK - 1][:])
-
+            nc.sync.dma_start(left[:, t, :], st[t][:, halves[0]])
+            nc.sync.dma_start(right[t][:], st[t][:, halves[1]])
         w2_bf = sb("w2_bf", [P, PACK, P, PACK], BF16)
-        for a in range(2):
-            deal(nc.scalar.copy, w2_bf, w2_raw, a)
+        deal(nc.scalar.copy, w2_bf, w2_raw, 0)
+        nc.scalar.copy(left[:, PACK - 1, :], st[PACK - 1][:, halves[0]])
+        nc.scalar.copy(right[PACK - 1][:], st[PACK - 1][:, halves[1]])
+        deal(nc.scalar.copy, w2_bf, w2_raw, 1)
+        st_copy = [[left[:, t, :], right[t][:]] for t in range(PACK)]
 
-        z32 = [sb("z32_%d" % a, [P, PACK, HALF], F32) for a in range(2)]
+        z32 = [sb("z32_%d" % a, [P, PACK, HALF], F32, tag=("z32", "left")[a]) for a in range(2)]
         z_bf = [sb("z_bf%d" % a, [P, HALF, PACK], BF16) for a in range(2)]
         for a in range(2):
             for t in range(PACK):
-                nc.vector.tensor_tensor(z32[a][:, t, :], st[t][:].indirect(n2_sb[:, list_halves[a]]), st_copy[t][:, halves[a]], SUB)
+                nc.vector.tensor_tensor(z32[a][:, t, :], st[t][:].indirect(n2_sb[:, list_halves[a]]), st_copy[t][a], SUB)
 
-        w2_codes = sb("w2_codes", [P, N], U32)
+        w2_codes = sb("w2_codes", [P, N], U32, tag="st3")
         w2_scales = sb("w2_scales", [P, N], U8)
         nc.vector.quantize_mx(
             out=w2_codes[:].bitcast(FP8X4), scales=w2_scales[:], in_=w2_bf[:].rearrange("p t m j -> p (t m j)")
@@ -163,26 +165,29 @@ def tile_picked_skipputbhop_none_p_kernel(
                 scales=z_scales[:, halves[a]],
                 in_=z_bf[a][:].rearrange("p c t -> p (c t)"),
             )
-            for t in (2 * a, 2 * a + 1):
+            for t in (range(1) if a == 0 else range(1, PACK)):
                 y_sb = sb("y_sb%d" % t, [P, S], F32, tag="st_copy%d" % t)
                 for bank, cols in y_parts[t]:
                     nc.scalar.copy(y_sb[:, cols], bank[:])
                 nc.vector.tensor_copy(y_picked[t][:], y_sb[:].indirect(n4_sb[:]))
 
         out_rows = out.rearrange("(p t) c -> p t c", t=PACK)
-        h_sb = [sb("h_sb%d" % t, [P, S], F32) for t in range(PACK)]
-        h_picked = [sb("h_picked%d" % t, [P, W], F32) for t in range(PACK)]
+        h_ps = []
         for t in range(PACK):
-            h_ps = psum.tile([P, S], F32, name="h_ps%d" % t, tag="bank%d" % ((5 + t) % 8))
-            product(h_ps[:], w2_codes[:, t * P : (t + 1) * P], w2_scales, t, z_codes[:], z_scales[:])
-            nc.scalar.copy(h_sb[t][:], h_ps[:])
+            h_ps.append(psum.tile([P, S], F32, name="h_ps%d" % t, tag="bank%d" % ((5 + t) % 8)))
+            product(h_ps[t][:], w2_codes[:, t * P : (t + 1) * P], w2_scales, t, z_codes[:], z_scales[:])
+        h_picked = [sb("h_picked%d" % t, [P, W], F32) for t in range(PACK)]
 
         def fetch(t):
-            nc.vector.tensor_scalar(h_picked[t][:], h_sb[t][:].indirect(n3_sb[:]), -0.5, 0.0, MULT, ADD)
+            h_sb = sb("h_sb%d" % t, [P, S], F32)
+            nc.scalar.copy(h_sb[:], h_ps[t][:])
+            nc.vector.tensor_scalar(h_picked[t][:], h_sb[:].indirect(n3_sb[:]), -0.5, 0.0, MULT, ADD)
 
         def put(t):
-            nc.vector.tensor_tensor(h_sb[t][:].indirect(n3_sb[:]), y_picked[t][:], h_picked[t][:], ADD)
-            nc.sync.dma_start(out_rows[:, t, :], h_sb[t][:])
+            out_sb = sb("out_sb%d" % t, [P, S], F32)
+            nc.scalar.copy(out_sb[:], h_ps[t][:])
+            nc.vector.tensor_tensor(out_sb[:].indirect(n3_sb[:]), y_picked[t][:], h_picked[t][:], ADD)
+            nc.sync.dma_start(out_rows[:, t, :], out_sb[:])
 
         fetch(0)
         for t in range(PACK):

from contextlib import ExitStack

import concourse.mybir as mybir

K, T, S, N, H, W = 512, 2048, 512, 512, 512, 256
FLOPS = 2 * K * H * S + 2 * H * N * S

F32 = mybir.dt.float32
BF16 = mybir.dt.bfloat16
I32 = mybir.dt.int32
U32 = mybir.dt.uint32
U16 = mybir.dt.uint16
U8 = mybir.dt.uint8
FP8X4 = mybir.dt.float8_e4m3fn_x4
COPY = mybir.ActivationFunctionType.Copy
ADD = mybir.AluOpType.add
SUB = mybir.AluOpType.subtract
MULT = mybir.AluOpType.mult

P = 128
PACK = 4
HALF = S // 2
LIST_HALF = HALF // 16


def tile_picked_skipputbhop_none_p_kernel(
    tc, x_words, x_scales, w1, gn, w2, offs, n1, n2, n3, n4, out
):
    nc = tc.nc
    halves = [slice(a * HALF, (a + 1) * HALF) for a in range(2)]
    list_halves = [slice(a * LIST_HALF, (a + 1) * LIST_HALF) for a in range(2)]
    with ExitStack() as ctx:
        keep = ctx.enter_context(tc.tile_pool(name="keep", bufs=1))
        psum = ctx.enter_context(tc.psum_pool(name="psum", bufs=1))

        def sb(name, shape, dtype, tag=None):
            return keep.tile(shape, dtype, name=name, tag=tag or name, align_bytes=64)

        def load_list(name, src):
            tile = keep.tile(list(src.shape), U16, name=name)
            nc.sync.dma_start(tile[:], src)
            return tile

        def deal(engine_copy, dealt, raw, a):
            engine_copy(
                dealt[:, :, a * (P // 2) : (a + 1) * (P // 2), :].rearrange("p t m j -> p m j t"),
                raw[:, :, halves[a]].rearrange("p j (m t) -> p m j t", t=PACK),
            )

        def product(acc, codes, scales, t, rhs_codes, rhs_scales):
            nc.tensor.matmul_mx(
                out=acc,
                lhsT=codes.bitcast(FP8X4),
                lhsT_scale=scales[:, t * P : (t + 1) * P],
                rhs=rhs_codes.bitcast(FP8X4),
                rhs_scale=rhs_scales,
                start=True,
                stop=True,
            )

        scale_rows = sb("scale_rows", [P, T], U8)
        nc.vector.memset(scale_rows[:].bitcast(I32), 0)
        for r in range(4):
            nc.sync.dma_start(scale_rows[r:P:32, :].bitcast(I32), x_scales[0, r:16:4, :].bitcast(I32))
        w1_raw = sb("w1_raw", [P, PACK, H], F32)
        nc.sync.dma_start(w1_raw[:], w1.rearrange("(p j) c -> p j c", j=PACK))
        offs_sb = load_list("offs_sb", offs)
        gain = sb("gain", [P, PACK], F32)
        nc.sync.dma_start(gain[:], gn.rearrange("(p t) o -> p (t o)", t=PACK))
        words = sb("words", [P, T], I32)
        nc.sync.dma_start(words[:], x_words[0].rearrange("p c r -> p (c r)").bitcast(I32))
        n1_sb = load_list("n1_sb", n1)
        w2_raw = sb("w2_raw", [P, PACK, N], F32)
        nc.sync.dma_start(w2_raw[:], w2.rearrange("(p j) c -> p j c", j=PACK))
        n2_sb = load_list("n2_sb", n2)
        n4_sb = load_list("n4_sb", n4)
        n3_sb = load_list("n3_sb", n3)

        w1_cols = w1_raw[:].rearrange("p j (m t) -> p m j t", t=PACK)
        w1_first = sb("w1_first", [P, P, PACK], BF16)
        nc.vector.tensor_copy(w1_first[:], w1_cols[:, :, :, 0])
        w1_rest = sb("w1_rest", [P, PACK - 1, P, PACK], BF16)
        nc.scalar.copy(w1_rest[:].rearrange("p t m j -> p m j t"), w1_cols[:, :, :, 1:PACK])
        w1_scales = sb("w1_scales", [P, H], U8)
        first_codes = sb("first_codes", [P, P], U32)
        nc.vector.quantize_mx(
            out=first_codes[:].bitcast(FP8X4), scales=w1_scales[:, 0:P], in_=w1_first[:].rearrange("p m j -> p (m j)")
        )
        x_bytes = sb("x_bytes", [P, S], U8, tag="w1_first")
        nc.vector.tensor_copy(x_bytes[:], scale_rows[:].indirect(offs_sb[:]))

        gain_neg = sb("gain_neg", [P, PACK], F32)
        gain_neg_half = sb("gain_neg_half", [P, PACK], F32)
        nc.scalar.activation(gain_neg[:], gain[:], COPY, scale=-1.0)
        nc.scalar.activation(gain_neg_half[:], gain[:], COPY, scale=-0.5)

        x_codes = sb("x_codes", [P, S], U32)
        for a in range(2):
            nc.vector.tensor_copy(x_codes[:, halves[a]], words[:].bitcast(U32).indirect(offs_sb[:, list_halves[a]]))

        rest_codes = sb("rest_codes", [P, H - P], U32, tag="words")
        w1_codes = [first_codes[:]] + [rest_codes[:, (t - 1) * P : t * P] for t in range(1, PACK)]
        for t in range(1, PACK):
            nc.vector.quantize_mx(
                out=w1_codes[t].bitcast(FP8X4),
                scales=w1_scales[:, t * P : (t + 1) * P],
                in_=w1_rest[:, t - 1, :, :].rearrange("p m j -> p (m j)"),
            )

        y_parts = []
        for t in range(PACK):
            spans = halves if t == 0 else [slice(0, S)]
            parts = []
            for a, cols in enumerate(spans):
                bank = psum.tile([P, cols.stop - cols.start], F32, name="y_ps%d_%d" % (t, a), tag="bank%d" % (t + PACK * a))
                product(bank[:], w1_codes[t], w1_scales, t, x_codes[:, cols], x_bytes[:, cols])
                parts.append((bank, cols))
            y_parts.append(parts)

        st = [sb("st%d" % t, [P, S], F32) for t in range(PACK)]
        for t in range(PACK):
            gy_half = sb("gy_half%d" % t, [P, S if t == 0 else 2 * S], F32)
            if t > 0:
                nc.vector.memset(gy_half[:, S:], 0.0)
            gy = sb("gy%d" % t, [P, S], F32)
            for bank, cols in y_parts[t]:
                nc.scalar.activation(gy_half[:, cols], bank[:], COPY, scale=gain_neg_half[:, t : t + 1])
                nc.scalar.activation(gy[:, cols], bank[:], COPY, scale=gain_neg[:, t : t + 1])
            for bank, cols in y_parts[t]:
                entries = slice(cols.start // 16, cols.stop // 16)
                nc.vector.tensor_tensor(st[t][:, cols], gy_half[:].indirect(n1_sb[:, entries]), gy[:, cols], ADD)
        left = sb("left", [P, PACK, HALF], F32)
        right = [sb("right%d" % t, [P, HALF], F32, tag="st_copy%d" % t) for t in range(PACK)]
        for t in range(PACK - 1):
            nc.sync.dma_start(left[:, t, :], st[t][:, halves[0]])
            nc.sync.dma_start(right[t][:], st[t][:, halves[1]])
        w2_bf = sb("w2_bf", [P, PACK, P, PACK], BF16)
        deal(nc.scalar.copy, w2_bf, w2_raw, 0)
        nc.scalar.copy(left[:, PACK - 1, :], st[PACK - 1][:, halves[0]])
        nc.scalar.copy(right[PACK - 1][:], st[PACK - 1][:, halves[1]])
        deal(nc.scalar.copy, w2_bf, w2_raw, 1)
        st_copy = [[left[:, t, :], right[t][:]] for t in range(PACK)]

        z32 = [sb("z32_%d" % a, [P, PACK, HALF], F32, tag=("z32", "left")[a]) for a in range(2)]
        z_bf = [sb("z_bf%d" % a, [P, HALF, PACK], BF16) for a in range(2)]
        for a in range(2):
            for t in range(PACK):
                nc.vector.tensor_tensor(z32[a][:, t, :], st[t][:].indirect(n2_sb[:, list_halves[a]]), st_copy[t][a], SUB)

        w2_codes = sb("w2_codes", [P, N], U32, tag="st3")
        w2_scales = sb("w2_scales", [P, N], U8)
        nc.vector.quantize_mx(
            out=w2_codes[:].bitcast(FP8X4), scales=w2_scales[:], in_=w2_bf[:].rearrange("p t m j -> p (t m j)")
        )

        z_codes = sb("z_codes", [P, S], U32)
        z_scales = sb("z_scales", [P, S], U8)
        y_picked = [sb("y_picked%d" % t, [P, W], F32) for t in range(PACK)]
        for a in range(2):
            nc.scalar.copy(
                z_bf[a][:].rearrange("p (c i) t -> p c t i", i=4), z32[a][:].rearrange("p t (c i) -> p c t i", i=4)
            )
            nc.vector.quantize_mx(
                out=z_codes[:, halves[a]].bitcast(FP8X4),
                scales=z_scales[:, halves[a]],
                in_=z_bf[a][:].rearrange("p c t -> p (c t)"),
            )
            for t in (range(1) if a == 0 else range(1, PACK)):
                y_sb = sb("y_sb%d" % t, [P, S], F32, tag="st_copy%d" % t)
                for bank, cols in y_parts[t]:
                    nc.scalar.copy(y_sb[:, cols], bank[:])
                nc.vector.tensor_copy(y_picked[t][:], y_sb[:].indirect(n4_sb[:]))

        out_rows = out.rearrange("(p t) c -> p t c", t=PACK)
        h_ps = []
        for t in range(PACK):
            h_ps.append(psum.tile([P, S], F32, name="h_ps%d" % t, tag="bank%d" % ((5 + t) % 8)))
            product(h_ps[t][:], w2_codes[:, t * P : (t + 1) * P], w2_scales, t, z_codes[:], z_scales[:])
        h_picked = [sb("h_picked%d" % t, [P, W], F32) for t in range(PACK)]

        def fetch(t):
            h_sb = sb("h_sb%d" % t, [P, S], F32)
            nc.scalar.copy(h_sb[:], h_ps[t][:])
            nc.vector.tensor_scalar(h_picked[t][:], h_sb[:].indirect(n3_sb[:]), -0.5, 0.0, MULT, ADD)

        def put(t):
            out_sb = sb("out_sb%d" % t, [P, S], F32)
            nc.scalar.copy(out_sb[:], h_ps[t][:])
            nc.vector.tensor_tensor(out_sb[:].indirect(n3_sb[:]), y_picked[t][:], h_picked[t][:], ADD)
            nc.sync.dma_start(out_rows[:, t, :], out_sb[:])

        fetch(0)
        for t in range(PACK):
            if t + 1 < PACK:
                fetch(t + 1)
            put(t)
